import numpy as np
import ml_dtypes

BF16 = ml_dtypes.bfloat16


def bf(x):
    return np.asarray(x, np.float32).astype(BF16)


def f32(x):
    return np.asarray(x, np.float32)


def f64(x):
    return np.asarray(x).astype(np.float64)


def striped(idx):
    return np.tile(idx.reshape(-1, 16).T, (8, 1))


S, K, M, N, E, Q = 1024, 128, 128, 1024, 8, 128


def setup_inputs():
    return {"table": bf(np.random.standard_normal((K, S))), "w": bf(np.random.standard_normal((E, K, M)) / np.sqrt(K)), "b": f32(0.5 * np.random.standard_normal((M, 1))), "offs": striped(np.sort(np.random.permutation(S).reshape(E, Q), axis=1).reshape(-1))}


def reference(table, w, b, offs):
    idx = offs[:16].T.reshape(-1)
    x = f64(table)[:, idx]
    y = np.concatenate([f64(w)[e].T @ x[:, e * Q : (e + 1) * Q] for e in range(E)], axis=1)
    return np.maximum(y + f64(b), 0.0)

@@ -1,0 +1,43 @@
+import concourse.mybir as mybir
+
+BF16, F32, U16 = mybir.dt.bfloat16, mybir.dt.float32, mybir.dt.uint16
+ADD, MAX = mybir.AluOpType.add, mybir.AluOpType.max
+
+P = 128
+S = 1024
+E = 8
+Q = 128
+
+FLOPS = 2 * P * P * E * Q
+
+HALF = S // 2
+PAIR = 2
+
+
+def tile_gather_matmul_kernel(tc, table, w, b, offs, out):
+    nc = tc.nc
+    with (
+        tc.tile_pool(name="held", bufs=1) as held,
+        tc.tile_pool(name="results", bufs=E) as results,
+        tc.psum_pool(name="psum", bufs=E) as psum,
+    ):
+        offsets = held.tile([P, E * Q // 16], U16, name="offsets")
+        nc.sync.dma_start(offsets[:], offs)
+        tokens = held.tile([P, S], BF16, name="tokens")
+        nc.scalar.dma_start(tokens[:, HALF:S], table[:, HALF:S])
+        nc.sync.dma_start(tokens[:, 0:HALF], table[:, 0:HALF])
+        bias = held.tile([P, 1], F32, name="bias")
+        nc.sync.dma_start(bias[:], b)
+        weights = []
+        for pair in range(E // PAIR):
+            both = held.tile([P, PAIR, P], BF16, name=f"weights{pair}")
+            nc.scalar.dma_start(both[:], w[pair * PAIR : (pair + 1) * PAIR].rearrange("e k m -> k e m"))
+            weights.append(both)
+
+        for e in range(E):
+            product = psum.tile([P, Q], F32, name="product")
+            picked = tokens[:].indirect(offsets[:, e * (Q // 16) : (e + 1) * (Q // 16)])
+            nc.tensor.matmul(product[:], weights[e // PAIR][:, e % PAIR, :], picked, start=True, stop=True)
+            result = results.tile([P, Q], F32, name="result")
+            nc.vector.tensor_scalar(result[:], product[:], bias[:, 0:1], 0.0, op0=ADD, op1=MAX)
+            nc.sync.dma_start(out[:, e * Q : (e + 1) * Q], result[:])

@@ -10,7 +10,6 @@ Q = 128
 
 FLOPS = 2 * P * P * E * Q
 
-HALF = S // 2
 PAIR = 2
 
 
@@ -24,20 +23,26 @@ def tile_gather_matmul_kernel(tc, table, w, b, offs, out):
         offsets = held.tile([P, E * Q // 16], U16, name="offsets")
         nc.sync.dma_start(offsets[:], offs)
         tokens = held.tile([P, S], BF16, name="tokens")
-        nc.scalar.dma_start(tokens[:, HALF:S], table[:, HALF:S])
-        nc.sync.dma_start(tokens[:, 0:HALF], table[:, 0:HALF])
+        nc.scalar.dma_start(tokens[:], table)
+        matrix = []
+        first = held.tile([P, P], BF16, name="first")
+        nc.sync.dma_start(first[:], w[0])
+        matrix.append(first[:])
         bias = held.tile([P, 1], F32, name="bias")
-        nc.sync.dma_start(bias[:], b)
-        weights = []
-        for pair in range(E // PAIR):
-            both = held.tile([P, PAIR, P], BF16, name=f"weights{pair}")
-            nc.scalar.dma_start(both[:], w[pair * PAIR : (pair + 1) * PAIR].rearrange("e k m -> k e m"))
-            weights.append(both)
+        nc.scalar.dma_start(bias[:], b)
+        second = held.tile([P, P], BF16, name="second")
+        nc.scalar.dma_start(second[:], w[1])
+        matrix.append(second[:])
+        for e in range(PAIR, E, PAIR):
+            both = held.tile([P, PAIR, P], BF16, name=f"weights{e}")
+            nc.scalar.dma_start(both[:], w[e : e + PAIR].rearrange("e k m -> k e m"))
+            for i in range(PAIR):
+                matrix.append(both[:, i, :])
 
         for e in range(E):
             product = psum.tile([P, Q], F32, name="product")
             picked = tokens[:].indirect(offsets[:, e * (Q // 16) : (e + 1) * (Q // 16)])
-            nc.tensor.matmul(product[:], weights[e // PAIR][:, e % PAIR, :], picked, start=True, stop=True)
+            nc.tensor.matmul(product[:], matrix[e], picked, start=True, stop=True)
             result = results.tile([P, Q], F32, name="result")
             nc.vector.tensor_scalar(result[:], product[:], bias[:, 0:1], 0.0, op0=ADD, op1=MAX)
             nc.sync.dma_start(out[:, e * Q : (e + 1) * Q], result[:])

@@ -17,7 +17,7 @@ def tile_gather_matmul_kernel(tc, table, w, b, offs, out):
     nc = tc.nc
     with (
         tc.tile_pool(name="held", bufs=1) as held,
-        tc.tile_pool(name="results", bufs=E) as results,
+        tc.tile_pool(name="results", bufs=E // PAIR) as results,
         tc.psum_pool(name="psum", bufs=E) as psum,
     ):
         offsets = held.tile([P, E * Q // 16], U16, name="offsets")
@@ -43,6 +43,8 @@ def tile_gather_matmul_kernel(tc, table, w, b, offs, out):
             product = psum.tile([P, Q], F32, name="product")
             picked = tokens[:].indirect(offsets[:, e * (Q // 16) : (e + 1) * (Q // 16)])
             nc.tensor.matmul(product[:], matrix[e], picked, start=True, stop=True)
-            result = results.tile([P, Q], F32, name="result")
-            nc.vector.tensor_scalar(result[:], product[:], bias[:, 0:1], 0.0, op0=ADD, op1=MAX)
-            nc.sync.dma_start(out[:, e * Q : (e + 1) * Q], result[:])
+            if e % PAIR == 0:
+                result = results.tile([P, PAIR * Q], F32, name="result")
+            nc.vector.tensor_scalar(result[:, (e % PAIR) * Q : (e % PAIR + 1) * Q], product[:], bias[:, 0:1], 0.0, op0=ADD, op1=MAX)
+            if e % PAIR == PAIR - 1:
+                nc.sync.dma_start(out[:, (e + 1 - PAIR) * Q : (e + 1) * Q], result[:])

@@ -11,6 +11,8 @@ Q = 128
 FLOPS = 2 * P * P * E * Q
 
 PAIR = 2
+SHARES = (1, 1, 2, 2, 1, 1)
+assert sum(SHARES) == E
 
 
 def tile_gather_matmul_kernel(tc, table, w, b, offs, out):
@@ -24,20 +26,19 @@ def tile_gather_matmul_kernel(tc, table, w, b, offs, out):
         nc.sync.dma_start(offsets[:], offs)
         tokens = held.tile([P, S], BF16, name="tokens")
         nc.scalar.dma_start(tokens[:], table)
-        matrix = []
-        first = held.tile([P, P], BF16, name="first")
-        nc.sync.dma_start(first[:], w[0])
-        matrix.append(first[:])
         bias = held.tile([P, 1], F32, name="bias")
-        nc.scalar.dma_start(bias[:], b)
-        second = held.tile([P, P], BF16, name="second")
-        nc.scalar.dma_start(second[:], w[1])
-        matrix.append(second[:])
-        for e in range(PAIR, E, PAIR):
-            both = held.tile([P, PAIR, P], BF16, name=f"weights{e}")
-            nc.scalar.dma_start(both[:], w[e : e + PAIR].rearrange("e k m -> k e m"))
-            for i in range(PAIR):
-                matrix.append(both[:, i, :])
+        matrix = []
+        for share in SHARES:
+            e = len(matrix)
+            group = held.tile([P, share, P], BF16, name=f"weights{e}")
+            if e == 0:
+                nc.sync.dma_start(group[:], w[e : e + share].rearrange("e k m -> k e m"))
+            else:
+                nc.scalar.dma_start(group[:], w[e : e + share].rearrange("e k m -> k e m"))
+            if e == 1:
+                nc.scalar.dma_start(bias[:], b)
+            for i in range(share):
+                matrix.append(group[:, i, :])
 
         for e in range(E):
             product = psum.tile([P, Q], F32, name="product")

@@ -22,21 +22,18 @@ def tile_gather_matmul_kernel(tc, table, w, b, offs, out):
         tc.tile_pool(name="results", bufs=E // PAIR) as results,
         tc.psum_pool(name="psum", bufs=E) as psum,
     ):
+        tokens = held.tile([P, S], BF16, name="tokens")
+        nc.sync.dma_start(tokens[:], table)
         offsets = held.tile([P, E * Q // 16], U16, name="offsets")
         nc.sync.dma_start(offsets[:], offs)
-        tokens = held.tile([P, S], BF16, name="tokens")
-        nc.scalar.dma_start(tokens[:], table)
         bias = held.tile([P, 1], F32, name="bias")
         matrix = []
         for share in SHARES:
             e = len(matrix)
             group = held.tile([P, share, P], BF16, name=f"weights{e}")
-            if e == 0:
-                nc.sync.dma_start(group[:], w[e : e + share].rearrange("e k m -> k e m"))
-            else:
-                nc.scalar.dma_start(group[:], w[e : e + share].rearrange("e k m -> k e m"))
+            nc.sync.dma_start(group[:], w[e : e + share].rearrange("e k m -> k e m"))
             if e == 1:
-                nc.scalar.dma_start(bias[:], b)
+                nc.sync.dma_start(bias[:], b)
             for i in range(share):
                 matrix.append(group[:, i, :])
 

@@ -11,7 +11,7 @@ Q = 128
 FLOPS = 2 * P * P * E * Q
 
 PAIR = 2
-SHARES = (1, 1, 2, 2, 1, 1)
+SHARES = (1, 2, 2, 2, 1)
 assert sum(SHARES) == E
 
 

import concourse.mybir as mybir

BF16, F32, U16 = mybir.dt.bfloat16, mybir.dt.float32, mybir.dt.uint16
ADD, MAX = mybir.AluOpType.add, mybir.AluOpType.max

P = 128
S = 1024
E = 8
Q = 128

FLOPS = 2 * P * P * E * Q

PAIR = 2
SHARES = (1, 2, 2, 2, 1)
assert sum(SHARES) == E


def tile_gather_matmul_kernel(tc, table, w, b, offs, out):
    nc = tc.nc
    with (
        tc.tile_pool(name="held", bufs=1) as held,
        tc.tile_pool(name="results", bufs=E // PAIR) as results,
        tc.psum_pool(name="psum", bufs=E) as psum,
    ):
        tokens = held.tile([P, S], BF16, name="tokens")
        nc.sync.dma_start(tokens[:], table)
        offsets = held.tile([P, E * Q // 16], U16, name="offsets")
        nc.sync.dma_start(offsets[:], offs)
        bias = held.tile([P, 1], F32, name="bias")
        matrix = []
        for share in SHARES:
            e = len(matrix)
            group = held.tile([P, share, P], BF16, name=f"weights{e}")
            nc.sync.dma_start(group[:], w[e : e + share].rearrange("e k m -> k e m"))
            if e == 1:
                nc.sync.dma_start(bias[:], b)
            for i in range(share):
                matrix.append(group[:, i, :])

        for e in range(E):
            product = psum.tile([P, Q], F32, name="product")
            picked = tokens[:].indirect(offsets[:, e * (Q // 16) : (e + 1) * (Q // 16)])
            nc.tensor.matmul(product[:], matrix[e], picked, start=True, stop=True)
            if e % PAIR == 0:
                result = results.tile([P, PAIR * Q], F32, name="result")
            nc.vector.tensor_scalar(result[:, (e % PAIR) * Q : (e % PAIR + 1) * Q], product[:], bias[:, 0:1], 0.0, op0=ADD, op1=MAX)
            if e % PAIR == PAIR - 1:
                nc.sync.dma_start(out[:, (e + 1 - PAIR) * Q : (e + 1) * Q], result[:])
